import numpy as np
import ml_dtypes


def mxq(x, axis, fmt="e4m3"):
    dtype, down = {"e4m3": (ml_dtypes.float8_e4m3fn, 7), "e5m2": (ml_dtypes.float8_e5m2, 14)}[fmt]
    v = np.moveaxis(np.asarray(x, np.float32).astype(ml_dtypes.bfloat16).astype(np.float64), axis, -1)
    blocks = v.reshape(v.shape[:-1] + (-1, 32))
    amax = np.abs(blocks).max(-1, keepdims=True)
    byte = np.maximum(np.where(amax > 0, np.frexp(amax)[1] - 1 + 127, 0) - down, 1)
    scale = np.exp2(byte - 127.0)
    codes = (blocks / scale).astype(np.float32).astype(dtype).astype(np.float64)
    return np.moveaxis((codes * scale).reshape(v.shape), -1, axis)


WIDE = False


def mx_kscale(k):
    if not WIDE:
        return np.ones(k)
    levels = np.array([10, -10, 5, -5, 0])
    if k % 512:
        return np.exp2(np.random.permutation(np.resize(levels, k // 32))).repeat(32)
    a = np.empty((k // 512, 16))
    for p in range(k // 512):
        a[p, :8] = np.random.permutation(np.resize(levels, 8))
        for g in range(8):
            far = levels[np.abs(levels - a[p, g]) >= 10]
            a[p, g + 8] = far[np.random.randint(len(far))]
    return np.exp2(a.ravel()).repeat(32)


def f64(x):
    return np.asarray(x).astype(np.float64)


def striped(idx):
    return np.tile(np.asarray(idx).reshape(-1, 16).T, (8, 1)).astype(np.uint16)


def unstriped(offs):
    return offs[:16].T.reshape(-1).astype(np.int64)


E2M1 = np.array([0.0, 0.5, 1.0, 1.5, 2.0, 3.0, 4.0, 6.0, -0.0, -0.5, -1.0, -1.5, -2.0, -3.0, -4.0, -6.0])


def pack_weight(w, fmt):
    k, n = w.shape
    w = f64(np.asarray(w, np.float32).astype(ml_dtypes.bfloat16)).reshape(k // 32, 32, n)
    amax = np.abs(w).max(1)
    if fmt == "e4m3":
        byte = np.frexp(amax)[1] - 1 + 127 - 7
    else:
        mant, ex = np.frexp(amax / 6.0)
        byte = np.where(mant > 0.5, ex, ex - 1) + 127
    byte = np.clip(np.where(amax > 0, byte, 1), 1, 254)
    scaled = (w * np.exp2(127.0 - byte)[:, None, :]).reshape(k, n).astype(np.float32)
    by_word = np.ascontiguousarray(scaled.reshape(k // 512, 128, 4, n).transpose(0, 1, 3, 2))
    if fmt == "e4m3":
        words = by_word.astype(ml_dtypes.float8_e4m3fn).view(np.uint8)
    else:
        c = by_word.astype(ml_dtypes.float4_e2m1fn).view(np.uint8) & 0xF
        words = (c[..., 0::2] | (c[..., 1::2] << 4)).reshape(k // 512, 128, 2 * n)
    return np.ascontiguousarray(words), np.ascontiguousarray(byte.astype(np.uint8).reshape(k // 512, 16, n))


def unpack_weight(words, scales, fmt):
    g, _, n = scales.shape
    words = np.ascontiguousarray(words).reshape(g, 128, n, -1)
    if fmt == "e4m3":
        vals = words.view(ml_dtypes.float8_e4m3fn).astype(np.float64)
    else:
        nib = np.empty((g, 128, n, 4), np.uint8)
        nib[..., 0::2] = words & 0xF
        nib[..., 1::2] = words >> 4
        vals = E2M1[nib]
    vals = vals * np.repeat(np.exp2(scales.astype(np.float64) - 127.0), 8, axis=1)[..., None]
    return vals.transpose(0, 1, 3, 2).reshape(g * 512, n)


def bf(x):
    return np.asarray(x, np.float32).astype(ml_dtypes.bfloat16)


def planes(Y):
    r, m = Y.shape
    b = f64(bf(Y)).reshape(r // 32, 32, m)
    amax = np.abs(b).max(1)
    byte = np.clip(np.where(amax > 0, np.frexp(amax)[1] - 1 + 127 - 7, 1), 1, 254)
    codes = (b * np.exp2(127.0 - byte)[:, None, :]).reshape(r, m).astype(np.float32).astype(ml_dtypes.float8_e4m3fn).view(np.uint8)
    words = codes.reshape(r // 512, 128, 4, m).transpose(0, 1, 3, 2)
    return np.ascontiguousarray(words), np.ascontiguousarray(byte.astype(np.uint8).reshape(r // 512, 16, m))


K, T, R, J, M = 512, 512, 2048, 512, 512


def setup_inputs():
    n = np.random.standard_normal
    idx = np.random.permutation(R)[:J]
    fk = mx_kscale(K)
    fj = mx_kscale(J)
    tj = np.ones(R)
    tj[idx] = fj
    xtp = pack_weight(n((K, T)) / fk[:, None], "e2m1")
    wup = pack_weight(n((K, R)) * 1 / np.sqrt(K) * fk[:, None] * tj, "e4m3")
    wyp = pack_weight(n((K, M)) * 1 / np.sqrt(K) * fk[:, None], "e2m1")
    return {
        "xt_words": xtp[0],
        "xt_scales": xtp[1],
        "wu_words": wup[0],
        "wu_scales": wup[1],
        "wd": (n((M, R)) * (1 / np.sqrt(J)) / tj).astype(np.float32),
        "wy_words": wyp[0],
        "wy_scales": wyp[1],
        "offs": striped(idx),
    }


def reference(xt_words, xt_scales, wu_words, wu_scales, wd, wy_words, wy_scales, offs):
    idx = unstriped(offs)
    xtu = unpack_weight(xt_words, xt_scales, "e2m1")
    wuu = unpack_weight(wu_words, wu_scales, "e4m3")
    wyu = unpack_weight(wy_words, wy_scales, "e2m1")
    wuidxg = wuu[:, idx]
    a = wuidxg.T @ xtu
    hid = np.maximum(a, 0.0)
    dj = f64(wd)[:, idx].T
    djq = mxq(dj, 0, "e4m3")
    hidq = mxq(hid, 0, "e4m3")
    y = djq.T @ hidq + wyu.T @ xtu
    words, scales = planes(y)
    return y, words, scales

@@ -1,0 +1,247 @@
+from contextlib import ExitStack
+
+import concourse.mybir as mybir
+from concourse.masks import make_identity
+
+K, T, R, J, M = 512, 512, 2048, 512, 512
+FLOPS = 3 * 2 * 512 * 512 * 512
+
+F32 = mybir.dt.float32
+BF16 = mybir.dt.bfloat16
+I32 = mybir.dt.int32
+U32 = mybir.dt.uint32
+U16 = mybir.dt.uint16
+U8 = mybir.dt.uint8
+FP8X4 = mybir.dt.float8_e4m3fn_x4
+FP4X4 = mybir.dt.float4_e2m1fn_x4
+ACT = mybir.ActivationFunctionType
+
+P = 128
+PACK = 4
+CHUNK = 128
+HALF = 256
+ROW_BYTES = 4 * R
+
+
+def load_scale_rows(queue, plane, scales):
+    for quad in range(4):
+        queue.dma_start(
+            out=plane[32 * quad : 32 * quad + 4, :].bitcast(I32),
+            in_=scales[0, 4 * quad : 4 * quad + 4, :].bitcast(I32),
+        )
+
+
+def tile_list_hot_neurons_pl_kernel(
+    tc, xt_words, xt_scales, wu_words, wu_scales, wd, wy_words, wy_scales, offs, out_0, out_1, out_2
+):
+    nc = tc.nc
+    with ExitStack() as ctx:
+        keep = ctx.enter_context(tc.tile_pool(name="keep", bufs=1))
+        wide = ctx.enter_context(tc.tile_pool(name="wide", bufs=1))
+        psum = ctx.enter_context(tc.psum_pool(name="psum", bufs=1))
+
+        offsets = keep.tile([P, J // 16], U16, name="offsets")
+        wu_table = keep.tile([P, R], I32, name="wu_table", align_bytes=64)
+        wu_plane = keep.tile([P, R], U8, name="wu_plane", align_bytes=64)
+        xt_codes = keep.tile([P, 2 * T], U8, name="xt_codes", align_bytes=64)
+        xt_plane = keep.tile([P, T], U8, name="xt_plane", align_bytes=64)
+        wy_raw = keep.tile([P, 2 * M], U8, name="wy_raw", align_bytes=64)
+        wy_raw_plane = keep.tile([P, M], U8, name="wy_raw_plane", align_bytes=64)
+        wd_rows = [wide.tile([P, R], F32, name="wd_rows%d" % t, align_bytes=64, offset=t * ROW_BYTES) for t in range(PACK)]
+        ident = keep.tile([P, P], F32, name="ident", align_bytes=64)
+
+        nc.vector.memset(wu_plane[:].bitcast(I32), 0)
+        nc.vector.memset(xt_plane[:].bitcast(I32), 0)
+        nc.vector.memset(wy_raw_plane[:].bitcast(I32), 0)
+
+        wd_dealt = wd.rearrange("(q t) r -> q t r", t=PACK)
+        nc.sync.dma_start(out=wu_table[:], in_=wu_words[0].rearrange("p n b -> p (n b)").bitcast(I32))
+        load_scale_rows(nc.sync, wu_plane, wu_scales)
+        nc.sync.dma_start(offsets[:], offs)
+        nc.sync.dma_start(out=xt_codes[:].bitcast(I32), in_=xt_words[0].bitcast(I32))
+        nc.sync.dma_start(out=wd_rows[0][:], in_=wd_dealt[:, 0, :])
+        load_scale_rows(nc.sync, xt_plane, xt_scales)
+        nc.sync.dma_start(out=wd_rows[1][:], in_=wd_dealt[:, 1, :])
+        nc.sync.dma_start(out=wy_raw[:].bitcast(I32), in_=wy_words[0].bitcast(I32))
+        load_scale_rows(nc.sync, wy_raw_plane, wy_scales)
+        for t in range(2, PACK):
+            nc.sync.dma_start(out=wd_rows[t][:], in_=wd_dealt[:, t, :])
+        make_identity(nc, ident[:])
+
+        wu_hot_plane = keep.tile([P, J], U8, name="wu_hot_plane", align_bytes=64)
+        wu_hot = keep.tile([P, J], U32, name="wu_hot", align_bytes=64)
+        nc.vector.tensor_copy(
+            out=wu_hot_plane[:].rearrange("p (i q) -> p q i", i=PACK), in_=wu_plane[:].indirect(offsets[:])
+        )
+        nc.vector.tensor_copy(
+            out=wu_hot[:].rearrange("p (i q) -> p q i", i=PACK), in_=wu_table[:].bitcast(U32).indirect(offsets[:])
+        )
+
+        hid_codes = [
+            keep.tile([P, HALF], U32, name="hid_codes0", align_bytes=64),
+            wide.tile([P, HALF], U32, name="hid_codes1", align_bytes=64, offset=2 * ROW_BYTES),
+        ]
+        hids = []
+        hid_plane = [keep.tile([P, HALF], U8, name="hid_plane%d" % g, align_bytes=64) for g in range(2)]
+        for g in range(2):
+            hid = keep.tile([P, HALF, PACK], BF16, name="hid%d" % g, align_bytes=64)
+            for c in range(2):
+                tok = g * HALF + c * CHUNK
+                a_bank = psum.tile([P, PACK, CHUNK], F32, name="a_bank%d%d" % (g, c), tag="bank%d%d" % (2 - g, c))
+                for i in range(PACK):
+                    nc.tensor.matmul_mx(
+                        out=a_bank[:, i, :],
+                        lhsT=wu_hot[:, i * P : (i + 1) * P].bitcast(FP8X4),
+                        lhsT_scale=wu_hot_plane[:, i * P : (i + 1) * P],
+                        rhs=xt_codes[:, 2 * tok : 2 * (tok + CHUNK)].bitcast(FP4X4),
+                        rhs_scale=xt_plane[:, tok : tok + CHUNK],
+                        start=True,
+                        stop=True,
+                    )
+                hid_part = hid[:, c * CHUNK : (c + 1) * CHUNK, :]
+                a_woven = a_bank[:].rearrange("p i n -> p n i")
+                nc.scalar.activation(out=hid_part, in_=a_woven, func=ACT.Relu)
+            hids.append(hid)
+
+        def quantise_hid(g):
+            nc.vector.quantize_mx(
+                out=hid_codes[g][:].bitcast(FP8X4), scales=hid_plane[g][:], in_=hids[g][:].rearrange("p n i -> p (n i)")
+            )
+
+        quantise_hid(0)
+
+        dj_codes = [
+            wide.tile([P, 2 * P], U32, name="dj_codes01", align_bytes=64, offset=2 * ROW_BYTES + 1024),
+            wide.tile([P, P], U32, name="dj_codes2", align_bytes=64, offset=3 * ROW_BYTES),
+            keep.tile([P, P], U32, name="dj_codes3", align_bytes=64),
+        ]
+        dj_plane = keep.tile([P, M], U8, name="dj_plane", align_bytes=64)
+        dj = [
+            wide.tile([P, 2 * P * PACK], BF16, name="dj01", align_bytes=64, offset=ROW_BYTES),
+            keep.tile([P, P * PACK], BF16, name="dj2", align_bytes=64),
+            keep.tile([P, P * PACK], BF16, name="dj3", align_bytes=64),
+        ]
+        dj_words = [dj_codes[0][:, :P], dj_codes[0][:, P:], dj_codes[1][:], dj_codes[2][:]]
+        dj_in = [dj[0][:, : P * PACK], dj[0][:, P * PACK :], dj[1][:], dj[2][:]]
+        turned = []
+
+        def pick_and_turn(t):
+            picked = keep.tile([P, J], BF16, name="picked%d" % t, align_bytes=64)
+            nc.vector.tensor_copy(out=picked[:, : J // 2], in_=wd_rows[t][:].indirect(offsets[:, : J // 32]))
+            nc.scalar.activation(
+                out=picked[:, J // 2 :], in_=wd_rows[t][:].indirect(offsets[:, J // 32 :]), func=ACT.Copy
+            )
+            pairs = picked[:].bitcast(F32)
+            bank = psum.tile([P, 2, P], F32, name="turned%d" % t, tag="bank2%d" % (t % 2))
+            for u in range(2):
+                nc.tensor.transpose(bank[:, u, :], pairs[:, u : J // 2 : 2], ident[:])
+            turned.append(bank)
+
+        def weave(t):
+            out = dj_in[t].bitcast(F32).rearrange("p (q u) -> p q u", u=2)
+            in_ = turned[t][:].rearrange("p u q -> p q u")
+            if t < 3:
+                nc.scalar.copy(out=out, in_=in_)
+            else:
+                nc.vector.tensor_copy(out=out, in_=in_)
+
+        def quantise_dj(n, first, count):
+            nc.vector.quantize_mx(
+                out=dj_codes[n][:].bitcast(FP8X4), scales=dj_plane[:, first * P : (first + count) * P], in_=dj[n][:]
+            )
+
+        pick_and_turn(0)
+        pick_and_turn(1)
+        weave(0)
+        wy_codes = keep.tile([P, 2 * M], U8, name="wy_codes", align_bytes=64)
+        wy_plane = keep.tile([P, M], U8, name="wy_plane", align_bytes=64)
+        nc.vector.tensor_copy(
+            out=wy_codes[:].bitcast(U16).rearrange("p (t q) -> p t q", t=PACK),
+            in_=wy_raw[:].bitcast(U16).rearrange("p (q t) -> p t q", t=PACK),
+        )
+        nc.vector.tensor_copy(
+            out=wy_plane[:].rearrange("p (t q) -> p t q", t=PACK),
+            in_=wy_raw_plane[:].rearrange("p (q t) -> p t q", t=PACK),
+        )
+
+        weave(1)
+        pick_and_turn(2)
+        quantise_hid(1)
+        quantise_dj(0, 0, 2)
+        weave(2)
+        pick_and_turn(3)
+        quantise_dj(1, 2, 1)
+        weave(3)
+        quantise_dj(2, 3, 1)
+
+        y_banks = [
+            [psum.tile([P, 2, HALF], F32, name="y_bank%d%d" % (h, g), tag="bank%d%d" % (h, g)) for g in range(2)]
+            for h in range(2)
+        ]
+        for t in range(PACK):
+            h, e = divmod(t, 2)
+            for g in range(2):
+                nc.tensor.matmul_mx(
+                    out=y_banks[h][g][:, e, :],
+                    lhsT=wy_codes[:, 2 * t * P : 2 * (t + 1) * P].bitcast(FP4X4),
+                    lhsT_scale=wy_plane[:, t * P : (t + 1) * P],
+                    rhs=xt_codes[:, 2 * g * HALF : 2 * (g + 1) * HALF].bitcast(FP4X4),
+                    rhs_scale=xt_plane[:, g * HALF : (g + 1) * HALF],
+                    start=(e == 0),
+                    stop=False,
+                )
+
+        y_woven = [keep.tile([P, HALF, PACK], BF16, name="y_woven%d" % g, align_bytes=64) for g in range(2)]
+        y_codes = keep.tile([P, T], U32, name="y_codes", align_bytes=64)
+        y_plane = keep.tile([P, T], U8, name="y_plane", align_bytes=64)
+        out_dealt = out_0.rearrange("(p t) n -> p t n", t=PACK)
+        out_words = out_1[0].rearrange("p n b -> p (n b)").bitcast(I32)
+
+        for h in range(2):
+            for e in range(2):
+                t = 2 * h + e
+                for g in range(2):
+                    nc.tensor.matmul_mx(
+                        out=y_banks[h][g][:, e, :],
+                        lhsT=dj_words[t].bitcast(FP8X4),
+                        lhsT_scale=dj_plane[:, t * P : (t + 1) * P],
+                        rhs=hid_codes[g][:].bitcast(FP8X4),
+                        rhs_scale=hid_plane[g][:],
+                        start=False,
+                        stop=(e == 1),
+                    )
+            planes = slice(2 * h, 2 * h + 2)
+            if h == 0:
+                y_rows = [
+                    wide.tile([P, 2, HALF], F32, name="y_rows0%d" % g, align_bytes=64, offset=3 * ROW_BYTES + 2048 * (g + 1))
+                    for g in range(2)
+                ]
+            else:
+                y_rows = [keep.tile([P, 2, HALF], F32, name="y_rows1%d" % g, align_bytes=64) for g in range(2)]
+            if h == 0:
+                nc.scalar.copy(out=y_rows[0][:], in_=y_banks[h][0][:])
+                nc.scalar.copy(out=y_rows[1][:], in_=y_banks[h][1][:])
+                nc.scalar.copy(out=y_woven[1][:, :, planes], in_=y_banks[h][1][:].rearrange("p e n -> p n e"))
+            else:
+                nc.vector.tensor_copy(out=y_rows[0][:], in_=y_banks[h][0][:])
+                nc.scalar.copy(out=y_woven[1][:, :, planes], in_=y_banks[h][1][:].rearrange("p e n -> p n e"))
+                nc.scalar.copy(out=y_rows[1][:], in_=y_banks[h][1][:])
+            nc.vector.tensor_copy(out=y_woven[0][:, :, planes], in_=y_rows[0][:].rearrange("p e n -> p n e"))
+            nc.sync.dma_start(out=out_dealt[:, planes, :HALF], in_=y_rows[0][:])
+            (nc.sync if h == 0 else nc.scalar).dma_start(out=out_dealt[:, planes, HALF:], in_=y_rows[1][:])
+
+        for g in range(2):
+            cols = slice(g * HALF, (g + 1) * HALF)
+            nc.vector.quantize_mx(
+                out=y_codes[:, cols].bitcast(FP8X4),
+                scales=y_plane[:, cols],
+                in_=y_woven[g][:].rearrange("p n t -> p (n t)"),
+            )
+            nc.sync.dma_start(out=out_words[:, cols], in_=y_codes[:, cols].bitcast(I32))
+
+        for quad in range(4):
+            queue = nc.sync if quad % 2 == 0 else nc.scalar
+            queue.dma_start(
+                out=out_2[0, 4 * quad : 4 * quad + 4, :].bitcast(I32),
+                in_=y_plane[32 * quad : 32 * quad + 4, :].bitcast(I32),
+            )

@@ -50,6 +50,9 @@ def tile_list_hot_neurons_pl_kernel(
         wd_rows = [wide.tile([P, R], F32, name="wd_rows%d" % t, align_bytes=64, offset=t * ROW_BYTES) for t in range(PACK)]
         ident = keep.tile([P, P], F32, name="ident", align_bytes=64)
 
+        warm = keep.tile([P, 2], F32, name="warm")
+        nc.vector.memset(warm[:, 0:1], 0.0)
+        nc.scalar.activation(out=warm[:, 1:2], in_=warm[:, 0:1], func=ACT.Relu)
         nc.vector.memset(wu_plane[:].bitcast(I32), 0)
         nc.vector.memset(xt_plane[:].bitcast(I32), 0)
         nc.vector.memset(wy_raw_plane[:].bitcast(I32), 0)

@@ -24,11 +24,8 @@ ROW_BYTES = 4 * R
 
 
 def load_scale_rows(queue, plane, scales):
-    for quad in range(4):
-        queue.dma_start(
-            out=plane[32 * quad : 32 * quad + 4, :].bitcast(I32),
-            in_=scales[0, 4 * quad : 4 * quad + 4, :].bitcast(I32),
-        )
+    for r in range(4):
+        queue.dma_start(out=plane[r:P:32, :].bitcast(I32), in_=scales[0, r:16:4, :].bitcast(I32))
 
 
 def tile_list_hot_neurons_pl_kernel(
@@ -169,8 +166,8 @@ def tile_list_hot_neurons_pl_kernel(
 
         weave(1)
         pick_and_turn(2)
-        quantise_hid(1)
         quantise_dj(0, 0, 2)
+        quantise_hid(1)
         weave(2)
         pick_and_turn(3)
         quantise_dj(1, 2, 1)
@@ -201,18 +198,18 @@ def tile_list_hot_neurons_pl_kernel(
         out_words = out_1[0].rearrange("p n b -> p (n b)").bitcast(I32)
 
         for h in range(2):
-            for e in range(2):
+            order = [(e, g) for g in range(2) for e in range(2)] if h == 0 else [(e, g) for e in range(2) for g in range(2)]
+            for e, g in order:
                 t = 2 * h + e
-                for g in range(2):
-                    nc.tensor.matmul_mx(
-                        out=y_banks[h][g][:, e, :],
-                        lhsT=dj_words[t].bitcast(FP8X4),
-                        lhsT_scale=dj_plane[:, t * P : (t + 1) * P],
-                        rhs=hid_codes[g][:].bitcast(FP8X4),
-                        rhs_scale=hid_plane[g][:],
-                        start=False,
-                        stop=(e == 1),
-                    )
+                nc.tensor.matmul_mx(
+                    out=y_banks[h][g][:, e, :],
+                    lhsT=dj_words[t].bitcast(FP8X4),
+                    lhsT_scale=dj_plane[:, t * P : (t + 1) * P],
+                    rhs=hid_codes[g][:].bitcast(FP8X4),
+                    rhs_scale=hid_plane[g][:],
+                    start=False,
+                    stop=(e == 1),
+                )
             planes = slice(2 * h, 2 * h + 2)
             if h == 0:
                 y_rows = [
@@ -242,9 +239,6 @@ def tile_list_hot_neurons_pl_kernel(
             )
             nc.sync.dma_start(out=out_words[:, cols], in_=y_codes[:, cols].bitcast(I32))
 
-        for quad in range(4):
-            queue = nc.sync if quad % 2 == 0 else nc.scalar
-            queue.dma_start(
-                out=out_2[0, 4 * quad : 4 * quad + 4, :].bitcast(I32),
-                in_=y_plane[32 * quad : 32 * quad + 4, :].bitcast(I32),
-            )
+        for r in range(4):
+            queue = nc.sync if r % 2 == 0 else nc.scalar
+            queue.dma_start(out=out_2[0, r:16:4, :].bitcast(I32), in_=y_plane[r:P:32, :].bitcast(I32))

from contextlib import ExitStack

import concourse.mybir as mybir
from concourse.masks import make_identity

K, T, R, J, M = 512, 512, 2048, 512, 512
FLOPS = 3 * 2 * 512 * 512 * 512

F32 = mybir.dt.float32
BF16 = mybir.dt.bfloat16
I32 = mybir.dt.int32
U32 = mybir.dt.uint32
U16 = mybir.dt.uint16
U8 = mybir.dt.uint8
FP8X4 = mybir.dt.float8_e4m3fn_x4
FP4X4 = mybir.dt.float4_e2m1fn_x4
ACT = mybir.ActivationFunctionType

P = 128
PACK = 4
CHUNK = 128
HALF = 256
ROW_BYTES = 4 * R


def load_scale_rows(queue, plane, scales):
    for r in range(4):
        queue.dma_start(out=plane[r:P:32, :].bitcast(I32), in_=scales[0, r:16:4, :].bitcast(I32))


def tile_list_hot_neurons_pl_kernel(
    tc, xt_words, xt_scales, wu_words, wu_scales, wd, wy_words, wy_scales, offs, out_0, out_1, out_2
):
    nc = tc.nc
    with ExitStack() as ctx:
        keep = ctx.enter_context(tc.tile_pool(name="keep", bufs=1))
        wide = ctx.enter_context(tc.tile_pool(name="wide", bufs=1))
        psum = ctx.enter_context(tc.psum_pool(name="psum", bufs=1))

        offsets = keep.tile([P, J // 16], U16, name="offsets")
        wu_table = keep.tile([P, R], I32, name="wu_table", align_bytes=64)
        wu_plane = keep.tile([P, R], U8, name="wu_plane", align_bytes=64)
        xt_codes = keep.tile([P, 2 * T], U8, name="xt_codes", align_bytes=64)
        xt_plane = keep.tile([P, T], U8, name="xt_plane", align_bytes=64)
        wy_raw = keep.tile([P, 2 * M], U8, name="wy_raw", align_bytes=64)
        wy_raw_plane = keep.tile([P, M], U8, name="wy_raw_plane", align_bytes=64)
        wd_rows = [wide.tile([P, R], F32, name="wd_rows%d" % t, align_bytes=64, offset=t * ROW_BYTES) for t in range(PACK)]
        ident = keep.tile([P, P], F32, name="ident", align_bytes=64)

        warm = keep.tile([P, 2], F32, name="warm")
        nc.vector.memset(warm[:, 0:1], 0.0)
        nc.scalar.activation(out=warm[:, 1:2], in_=warm[:, 0:1], func=ACT.Relu)
        nc.vector.memset(wu_plane[:].bitcast(I32), 0)
        nc.vector.memset(xt_plane[:].bitcast(I32), 0)
        nc.vector.memset(wy_raw_plane[:].bitcast(I32), 0)

        wd_dealt = wd.rearrange("(q t) r -> q t r", t=PACK)
        nc.sync.dma_start(out=wu_table[:], in_=wu_words[0].rearrange("p n b -> p (n b)").bitcast(I32))
        load_scale_rows(nc.sync, wu_plane, wu_scales)
        nc.sync.dma_start(offsets[:], offs)
        nc.sync.dma_start(out=xt_codes[:].bitcast(I32), in_=xt_words[0].bitcast(I32))
        nc.sync.dma_start(out=wd_rows[0][:], in_=wd_dealt[:, 0, :])
        load_scale_rows(nc.sync, xt_plane, xt_scales)
        nc.sync.dma_start(out=wd_rows[1][:], in_=wd_dealt[:, 1, :])
        nc.sync.dma_start(out=wy_raw[:].bitcast(I32), in_=wy_words[0].bitcast(I32))
        load_scale_rows(nc.sync, wy_raw_plane, wy_scales)
        for t in range(2, PACK):
            nc.sync.dma_start(out=wd_rows[t][:], in_=wd_dealt[:, t, :])
        make_identity(nc, ident[:])

        wu_hot_plane = keep.tile([P, J], U8, name="wu_hot_plane", align_bytes=64)
        wu_hot = keep.tile([P, J], U32, name="wu_hot", align_bytes=64)
        nc.vector.tensor_copy(
            out=wu_hot_plane[:].rearrange("p (i q) -> p q i", i=PACK), in_=wu_plane[:].indirect(offsets[:])
        )
        nc.vector.tensor_copy(
            out=wu_hot[:].rearrange("p (i q) -> p q i", i=PACK), in_=wu_table[:].bitcast(U32).indirect(offsets[:])
        )

        hid_codes = [
            keep.tile([P, HALF], U32, name="hid_codes0", align_bytes=64),
            wide.tile([P, HALF], U32, name="hid_codes1", align_bytes=64, offset=2 * ROW_BYTES),
        ]
        hids = []
        hid_plane = [keep.tile([P, HALF], U8, name="hid_plane%d" % g, align_bytes=64) for g in range(2)]
        for g in range(2):
            hid = keep.tile([P, HALF, PACK], BF16, name="hid%d" % g, align_bytes=64)
            for c in range(2):
                tok = g * HALF + c * CHUNK
                a_bank = psum.tile([P, PACK, CHUNK], F32, name="a_bank%d%d" % (g, c), tag="bank%d%d" % (2 - g, c))
                for i in range(PACK):
                    nc.tensor.matmul_mx(
                        out=a_bank[:, i, :],
                        lhsT=wu_hot[:, i * P : (i + 1) * P].bitcast(FP8X4),
                        lhsT_scale=wu_hot_plane[:, i * P : (i + 1) * P],
                        rhs=xt_codes[:, 2 * tok : 2 * (tok + CHUNK)].bitcast(FP4X4),
                        rhs_scale=xt_plane[:, tok : tok + CHUNK],
                        start=True,
                        stop=True,
                    )
                hid_part = hid[:, c * CHUNK : (c + 1) * CHUNK, :]
                a_woven = a_bank[:].rearrange("p i n -> p n i")
                nc.scalar.activation(out=hid_part, in_=a_woven, func=ACT.Relu)
            hids.append(hid)

        def quantise_hid(g):
            nc.vector.quantize_mx(
                out=hid_codes[g][:].bitcast(FP8X4), scales=hid_plane[g][:], in_=hids[g][:].rearrange("p n i -> p (n i)")
            )

        quantise_hid(0)

        dj_codes = [
            wide.tile([P, 2 * P], U32, name="dj_codes01", align_bytes=64, offset=2 * ROW_BYTES + 1024),
            wide.tile([P, P], U32, name="dj_codes2", align_bytes=64, offset=3 * ROW_BYTES),
            keep.tile([P, P], U32, name="dj_codes3", align_bytes=64),
        ]
        dj_plane = keep.tile([P, M], U8, name="dj_plane", align_bytes=64)
        dj = [
            wide.tile([P, 2 * P * PACK], BF16, name="dj01", align_bytes=64, offset=ROW_BYTES),
            keep.tile([P, P * PACK], BF16, name="dj2", align_bytes=64),
            keep.tile([P, P * PACK], BF16, name="dj3", align_bytes=64),
        ]
        dj_words = [dj_codes[0][:, :P], dj_codes[0][:, P:], dj_codes[1][:], dj_codes[2][:]]
        dj_in = [dj[0][:, : P * PACK], dj[0][:, P * PACK :], dj[1][:], dj[2][:]]
        turned = []

        def pick_and_turn(t):
            picked = keep.tile([P, J], BF16, name="picked%d" % t, align_bytes=64)
            nc.vector.tensor_copy(out=picked[:, : J // 2], in_=wd_rows[t][:].indirect(offsets[:, : J // 32]))
            nc.scalar.activation(
                out=picked[:, J // 2 :], in_=wd_rows[t][:].indirect(offsets[:, J // 32 :]), func=ACT.Copy
            )
            pairs = picked[:].bitcast(F32)
            bank = psum.tile([P, 2, P], F32, name="turned%d" % t, tag="bank2%d" % (t % 2))
            for u in range(2):
                nc.tensor.transpose(bank[:, u, :], pairs[:, u : J // 2 : 2], ident[:])
            turned.append(bank)

        def weave(t):
            out = dj_in[t].bitcast(F32).rearrange("p (q u) -> p q u", u=2)
            in_ = turned[t][:].rearrange("p u q -> p q u")
            if t < 3:
                nc.scalar.copy(out=out, in_=in_)
            else:
                nc.vector.tensor_copy(out=out, in_=in_)

        def quantise_dj(n, first, count):
            nc.vector.quantize_mx(
                out=dj_codes[n][:].bitcast(FP8X4), scales=dj_plane[:, first * P : (first + count) * P], in_=dj[n][:]
            )

        pick_and_turn(0)
        pick_and_turn(1)
        weave(0)
        wy_codes = keep.tile([P, 2 * M], U8, name="wy_codes", align_bytes=64)
        wy_plane = keep.tile([P, M], U8, name="wy_plane", align_bytes=64)
        nc.vector.tensor_copy(
            out=wy_codes[:].bitcast(U16).rearrange("p (t q) -> p t q", t=PACK),
            in_=wy_raw[:].bitcast(U16).rearrange("p (q t) -> p t q", t=PACK),
        )
        nc.vector.tensor_copy(
            out=wy_plane[:].rearrange("p (t q) -> p t q", t=PACK),
            in_=wy_raw_plane[:].rearrange("p (q t) -> p t q", t=PACK),
        )

        weave(1)
        pick_and_turn(2)
        quantise_dj(0, 0, 2)
        quantise_hid(1)
        weave(2)
        pick_and_turn(3)
        quantise_dj(1, 2, 1)
        weave(3)
        quantise_dj(2, 3, 1)

        y_banks = [
            [psum.tile([P, 2, HALF], F32, name="y_bank%d%d" % (h, g), tag="bank%d%d" % (h, g)) for g in range(2)]
            for h in range(2)
        ]
        for t in range(PACK):
            h, e = divmod(t, 2)
            for g in range(2):
                nc.tensor.matmul_mx(
                    out=y_banks[h][g][:, e, :],
                    lhsT=wy_codes[:, 2 * t * P : 2 * (t + 1) * P].bitcast(FP4X4),
                    lhsT_scale=wy_plane[:, t * P : (t + 1) * P],
                    rhs=xt_codes[:, 2 * g * HALF : 2 * (g + 1) * HALF].bitcast(FP4X4),
                    rhs_scale=xt_plane[:, g * HALF : (g + 1) * HALF],
                    start=(e == 0),
                    stop=False,
                )

        y_woven = [keep.tile([P, HALF, PACK], BF16, name="y_woven%d" % g, align_bytes=64) for g in range(2)]
        y_codes = keep.tile([P, T], U32, name="y_codes", align_bytes=64)
        y_plane = keep.tile([P, T], U8, name="y_plane", align_bytes=64)
        out_dealt = out_0.rearrange("(p t) n -> p t n", t=PACK)
        out_words = out_1[0].rearrange("p n b -> p (n b)").bitcast(I32)

        for h in range(2):
            order = [(e, g) for g in range(2) for e in range(2)] if h == 0 else [(e, g) for e in range(2) for g in range(2)]
            for e, g in order:
                t = 2 * h + e
                nc.tensor.matmul_mx(
                    out=y_banks[h][g][:, e, :],
                    lhsT=dj_words[t].bitcast(FP8X4),
                    lhsT_scale=dj_plane[:, t * P : (t + 1) * P],
                    rhs=hid_codes[g][:].bitcast(FP8X4),
                    rhs_scale=hid_plane[g][:],
                    start=False,
                    stop=(e == 1),
                )
            planes = slice(2 * h, 2 * h + 2)
            if h == 0:
                y_rows = [
                    wide.tile([P, 2, HALF], F32, name="y_rows0%d" % g, align_bytes=64, offset=3 * ROW_BYTES + 2048 * (g + 1))
                    for g in range(2)
                ]
            else:
                y_rows = [keep.tile([P, 2, HALF], F32, name="y_rows1%d" % g, align_bytes=64) for g in range(2)]
            if h == 0:
                nc.scalar.copy(out=y_rows[0][:], in_=y_banks[h][0][:])
                nc.scalar.copy(out=y_rows[1][:], in_=y_banks[h][1][:])
                nc.scalar.copy(out=y_woven[1][:, :, planes], in_=y_banks[h][1][:].rearrange("p e n -> p n e"))
            else:
                nc.vector.tensor_copy(out=y_rows[0][:], in_=y_banks[h][0][:])
                nc.scalar.copy(out=y_woven[1][:, :, planes], in_=y_banks[h][1][:].rearrange("p e n -> p n e"))
                nc.scalar.copy(out=y_rows[1][:], in_=y_banks[h][1][:])
            nc.vector.tensor_copy(out=y_woven[0][:, :, planes], in_=y_rows[0][:].rearrange("p e n -> p n e"))
            nc.sync.dma_start(out=out_dealt[:, planes, :HALF], in_=y_rows[0][:])
            (nc.sync if h == 0 else nc.scalar).dma_start(out=out_dealt[:, planes, HALF:], in_=y_rows[1][:])

        for g in range(2):
            cols = slice(g * HALF, (g + 1) * HALF)
            nc.vector.quantize_mx(
                out=y_codes[:, cols].bitcast(FP8X4),
                scales=y_plane[:, cols],
                in_=y_woven[g][:].rearrange("p n t -> p (n t)"),
            )
            nc.sync.dma_start(out=out_words[:, cols], in_=y_codes[:, cols].bitcast(I32))

        for r in range(4):
            queue = nc.sync if r % 2 == 0 else nc.scalar
            queue.dma_start(out=out_2[0, r:16:4, :].bitcast(I32), in_=y_plane[r:P:32, :].bitcast(I32))
